import numpy as np
import ml_dtypes


def mxq(x, axis, fmt="e4m3"):
    dtype, down = {"e4m3": (ml_dtypes.float8_e4m3fn, 7), "e5m2": (ml_dtypes.float8_e5m2, 14)}[fmt]
    v = np.moveaxis(np.asarray(x, np.float32).astype(ml_dtypes.bfloat16).astype(np.float64), axis, -1)
    blocks = v.reshape(v.shape[:-1] + (-1, 32))
    amax = np.abs(blocks).max(-1, keepdims=True)
    byte = np.maximum(np.where(amax > 0, np.frexp(amax)[1] - 1 + 127, 0) - down, 1)
    scale = np.exp2(byte - 127.0)
    codes = (blocks / scale).astype(np.float32).astype(dtype).astype(np.float64)
    return np.moveaxis((codes * scale).reshape(v.shape), -1, axis)


WIDE = False


def mx_kscale(k):
    if not WIDE:
        return np.ones(k)
    levels = np.array([10, -10, 5, -5, 0])
    if k % 512:
        return np.exp2(np.random.permutation(np.resize(levels, k // 32))).repeat(32)
    a = np.empty((k // 512, 16))
    for p in range(k // 512):
        a[p, :8] = np.random.permutation(np.resize(levels, 8))
        for g in range(8):
            far = levels[np.abs(levels - a[p, g]) >= 10]
            a[p, g + 8] = far[np.random.randint(len(far))]
    return np.exp2(a.ravel()).repeat(32)


BF16 = ml_dtypes.bfloat16


def bf(x):
    return np.asarray(x, np.float32).astype(BF16)


def f64(x):
    return np.asarray(x).astype(np.float64)


E2M1 = np.array([0.0, 0.5, 1.0, 1.5, 2.0, 3.0, 4.0, 6.0, -0.0, -0.5, -1.0, -1.5, -2.0, -3.0, -4.0, -6.0])


def pack_weight(w, fmt):
    k, n = w.shape
    w = f64(bf(w)).reshape(k // 32, 32, n)
    amax = np.abs(w).max(1)
    if fmt == "e4m3":
        byte = np.frexp(amax)[1] - 1 + 127 - 7
    else:
        mant, ex = np.frexp(amax / 6.0)
        byte = np.where(mant > 0.5, ex, ex - 1) + 127
    byte = np.clip(np.where(amax > 0, byte, 1), 1, 254)
    scaled = (w * np.exp2(127.0 - byte)[:, None, :]).reshape(k, n).astype(np.float32)
    by_word = np.ascontiguousarray(scaled.reshape(k // 512, 128, 4, n).transpose(0, 1, 3, 2))
    if fmt == "e4m3":
        words = by_word.astype(ml_dtypes.float8_e4m3fn).view(np.uint8)
    else:
        c = by_word.astype(ml_dtypes.float4_e2m1fn).view(np.uint8) & 0xF
        words = c[..., 0::2] | (c[..., 1::2] << 4)
    return np.ascontiguousarray(words), np.ascontiguousarray(byte.astype(np.uint8).reshape(k // 512, 16, n))


def unpack_weight(words, scales, fmt):
    g, p, n, _ = words.shape
    if fmt == "e4m3":
        vals = np.ascontiguousarray(words).view(ml_dtypes.float8_e4m3fn).astype(np.float64)
    else:
        nib = np.empty((g, p, n, 4), np.uint8)
        nib[..., 0::2] = words & 0xF
        nib[..., 1::2] = words >> 4
        vals = E2M1[nib]
    vals = vals * np.repeat(np.exp2(scales.astype(np.float64) - 127.0), 8, axis=1)[..., None]
    return vals.transpose(0, 1, 3, 2).reshape(g * 512, n)
def pack4(w):
    words, scales = pack_weight(w, "e2m1")
    return words.reshape(words.shape[0], 128, -1), scales


def unpack4(words, scales):
    return unpack_weight(words.reshape(words.shape[0], 128, -1, 2), scales, "e2m1")


V, C, J, F, L, S = 512, 4, 512, 1536, 1024, 512


def setup_inputs():
    a, u = mx_kscale(J), mx_kscale(L)
    t = mx_kscale(C * V)
    t_vertex = t.reshape(V, C)[:, 0]
    basis = np.random.standard_normal((L, C * V)) * u[:, None] / t
    codes = np.random.standard_normal((L, S)) / np.sqrt(L) / u[:, None]
    basis_words, basis_scales = pack4(basis)
    codes_words, codes_scales = pack4(codes)
    return {"skin": bf(np.abs(np.random.standard_normal((V, J))) / np.sqrt(J) * a),
            "bones": bf(np.random.standard_normal((J, C * F)) / a[:, None]),
            "mass": bf(np.random.uniform(0.5, 1.5, V) / np.sqrt(C * V) * t_vertex),
            "basis_words": basis_words, "basis_scales": basis_scales,
            "codes_words": codes_words, "codes_scales": codes_scales,
            "template": bf(0.5 * np.random.standard_normal(C * V) / t),
            "shift": bf(0.5 * np.random.standard_normal(F))}


def reference(skin, bones, mass, basis_words, basis_scales, codes_words, codes_scales, template, shift):
    blend = mxq(f64(skin), 1, "e4m3") @ mxq(f64(bones), 0, "e4m3")
    moved = (blend * f64(mass)[:, None]).reshape(C * V, F)
    d = unpack4(basis_words, basis_scales)
    z = unpack4(codes_words, codes_scales)
    rest = (d.T @ z) + f64(template)[:, None]
    centre = mxq(moved, 0, "e4m3").T @ mxq(rest, 0, "e4m3")
    return centre + f64(shift)[:, None]

@@ -1,0 +1,338 @@
+from contextlib import ExitStack
+
+import concourse.mybir as mybir
+from concourse.masks import make_identity
+
+V, C, J, F, L, S = 512, 4, 512, 1536, 1024, 512
+FLOPS = 2 * V * J * C * F + 2 * L * C * V * S + 2 * C * V * F * S
+
+F32 = mybir.dt.float32
+BF16 = mybir.dt.bfloat16
+I32 = mybir.dt.int32
+U32 = mybir.dt.uint32
+U8 = mybir.dt.uint8
+FP8X4 = mybir.dt.float8_e4m3fn_x4
+FP4X4 = mybir.dt.float4_e2m1fn_x4
+ACT = mybir.ActivationFunctionType
+ALU = mybir.AluOpType
+
+P = 128
+BANK = 512
+N_BANKS = 8
+GROUPS = V // P
+TILES = F // P
+CHUNK = 2 * P
+CHUNKS = F // CHUNK
+L_PASSES = L // (4 * P)
+UNITS = 2 * GROUPS
+
+
+def tile_skinned_mass_moments_s12_kernel(
+    tc, skin, bones, mass, basis_words, basis_scales, codes_words, codes_scales, template, shift, out
+):
+    nc = tc.nc
+    with ExitStack() as ctx:
+        keep = ctx.enter_context(tc.tile_pool(name="keep", bufs=1))
+        work = ctx.enter_context(tc.tile_pool(name="work", bufs=1))
+        psum = ctx.enter_context(tc.psum_pool(name="psum", bufs=1))
+        ctx.enter_context(tc.manual_schedule())
+
+        banks_taken = []
+
+        def next_bank():
+            n = len(banks_taken)
+            bank = psum.tile([P, BANK], F32, name=f"bank{n}", tag=f"bank{n % N_BANKS}")
+            banks_taken.append(bank)
+            return bank
+
+        def kept(name, shape, dtype):
+            return keep.tile(shape, dtype, name=name, tag=name, align_bytes=64)
+
+        def rotating(tag, n, shape, dtype, bufs):
+            return work.tile(shape, dtype, name=f"{tag}{n}", tag=tag, bufs=bufs, align_bytes=64)
+
+        def quantize(codes, scales, values):
+            nc.vector.quantize_mx(out=codes.bitcast(FP8X4), scales=scales, in_=values)
+
+        z_scales = kept("z_scales", [P, L_PASSES, S], U8)
+        d_scales = kept("d_scales", [P, L_PASSES, C * V], U8)
+        nc.vector.memset(z_scales[:].bitcast(I32), 0)
+        nc.vector.memset(d_scales[:].bitcast(I32), 0)
+        ident = kept("ident", [P, P], F32)
+        make_identity(nc, ident[:])
+        rows_f32 = kept("rows_f32", [P, P], F32)
+        nc.gpsimd.memset(rows_f32[:], 0.0)
+
+        skin_raw = [kept(f"skin_raw{h}", [P, 2, J], BF16) for h in range(2)]
+        bones_raw = [[kept(f"bones_raw{ch}_{c}", [P, 4, CHUNK], BF16) for c in range(C)] for ch in range(CHUNKS)]
+        rows_bf = kept("rows_bf", [GROUPS + TILES, P], BF16)
+        templ_cols = kept("templ_cols", [P, GROUPS, C], BF16)
+        z_words = kept("z_words", [P, L_PASSES, 2 * S], U8)
+        d_words = [kept(f"d_words{g}", [P, L_PASSES, 2 * BANK], U8) for g in range(GROUPS)]
+        bones_view = bones.rearrange("(p t) (c f) -> p t c f", t=4, c=C)
+
+        def load_skin(h):
+            nc.sync.dma_start(
+                out=skin_raw[h][:], in_=skin[2 * P * h : 2 * P * (h + 1), :].rearrange("(g p) j -> p g j", p=P)
+            )
+
+        def load_bones(ch):
+            for c in range(C):
+                nc.sync.dma_start(out=bones_raw[ch][c][:], in_=bones_view[:, :, c, CHUNK * ch : CHUNK * (ch + 1)])
+
+        def load_scale_rows(plane, rows):
+            for q in range(4):
+                nc.sync.dma_start(
+                    out=plane[32 * q : 32 * q + 4].bitcast(I32),
+                    in_=rows.bitcast(I32)[:, 4 * q : 4 * q + 4, :].rearrange("l r n -> r l n"),
+                )
+
+        def load_basis(g):
+            nc.sync.dma_start(
+                out=d_words[g][:].bitcast(I32),
+                in_=basis_words.bitcast(I32)[:, :, 256 * g : 256 * (g + 1)].rearrange("l p n -> p l n"),
+            )
+
+        def load_small():
+            nc.scalar.dma_start(out=rows_bf[0:GROUPS, :], in_=mass.rearrange("(g p) -> g p", p=P))
+            nc.scalar.dma_start(out=rows_bf[GROUPS:, :], in_=shift.rearrange("(i p) -> i p", p=P))
+            nc.scalar.dma_start(out=templ_cols[:], in_=template.rearrange("(g p c) -> p g c", p=P, c=C))
+
+        def load_codes():
+            load_scale_rows(z_scales, codes_scales)
+            nc.sync.dma_start(out=z_words[:].bitcast(I32), in_=codes_words.bitcast(I32).rearrange("l p n -> p l n"))
+            load_scale_rows(d_scales, basis_scales)
+
+        load_skin(0)
+        load_small()
+        load_bones(0)
+        load_skin(1)
+        load_codes()
+        load_basis(0)
+        load_bones(1)
+        load_basis(1)
+        load_basis(2)
+        load_basis(3)
+        load_bones(2)
+        load_bones(3)
+        load_bones(4)
+        load_bones(5)
+
+        skin_grouped = [kept(f"skin_grouped{h}", [P, 2 * P * 4], BF16) for h in range(2)]
+        skin_codes = [kept(f"skin_codes{h}", [P, 2 * P], U32) for h in range(2)]
+        skin_scales = [kept(f"skin_scales{h}", [P, 2 * P], U8) for h in range(2)]
+
+        def turn_skin(h):
+            bank = next_bank()
+            words = skin_raw[h][:].bitcast(F32)
+            for g in range(2):
+                for u in range(2):
+                    col = P * (2 * g + u)
+                    nc.tensor.transpose(bank[:, col : col + P], words[:, g, u : 2 * P : 2], ident[:])
+            nc.scalar.copy(
+                out=skin_grouped[h][:].bitcast(F32).rearrange("p (g v u) -> p g v u", g=2, u=2),
+                in_=bank[:].rearrange("p (g u v) -> p g v u", g=2, u=2),
+            )
+
+        def quantize_skin(h):
+            quantize(skin_codes[h][:], skin_scales[h][:], skin_grouped[h][:])
+
+        cols = kept("cols", [P, GROUPS + TILES], F32)
+
+        def turn_mass_and_shift():
+            nc.scalar.copy(out=rows_f32[0 : GROUPS + TILES, :], in_=rows_bf[:])
+            bank = next_bank()
+            nc.tensor.transpose(bank[:, 0:P], rows_f32[:], ident[:])
+            nc.scalar.copy(out=cols[:], in_=bank[:, 0 : GROUPS + TILES])
+
+        templ_rows = [kept(f"templ_rows{h}", [P, 2, BANK], BF16) for h in range(2)]
+
+        def spread_template(h):
+            bank = next_bank()
+            words = templ_cols[:].rearrange("p g c -> p (g c)").bitcast(F32)
+            for n in range(4):
+                w = 4 * h + n
+                nc.tensor.transpose(bank[:, P * n : P * (n + 1)], words[:, w : w + 1].to_broadcast([P, P]), ident[:])
+            nc.scalar.copy(out=templ_rows[h][:].rearrange("p g k -> p (g k)").bitcast(F32), in_=bank[:])
+
+        grouped = {}
+        bones_q = {}
+
+        def interleave(n, on_scalar):
+            ch, c = divmod(n, C)
+            if c == 0:
+                grouped[ch] = rotating("grouped", ch, [P, 2, C, P * 4], BF16, 3)
+            dst = grouped[ch][:, :, c, :].rearrange("p i (f t) -> p i f t", t=4)
+            src = bones_raw[ch][c][:].rearrange("p t (i f) -> p i f t", i=2)
+            if on_scalar:
+                nc.scalar.copy(out=dst, in_=src)
+            else:
+                nc.vector.tensor_copy(out=dst, in_=src)
+
+        def quantize_bones(i):
+            codes = rotating("bones_codes", i, [P, BANK], U32, 4)
+            scales = rotating("bones_scales", i, [P, BANK], U8, 4)
+            quantize(codes[:], scales[:], grouped[i // 2][:, i % 2].rearrange("p c w -> p (c w)"))
+            bones_q[i] = (codes, scales)
+
+        moved = {}
+        moved_q = {}
+
+        def blend(i, g, on_vector):
+            if g == 0:
+                moved[i] = rotating("moved", i, [P, GROUPS, BANK], BF16, 3)
+            bank = next_bank()
+            v = slice(P * (g % 2), P * (g % 2 + 1))
+            nc.tensor.matmul_mx(
+                out=bank[:],
+                lhsT=skin_codes[g // 2][:, v].bitcast(FP8X4),
+                lhsT_scale=skin_scales[g // 2][:, v],
+                rhs=bones_q[i][0][:].bitcast(FP8X4),
+                rhs_scale=bones_q[i][1][:],
+                start=True,
+                stop=True,
+            )
+            dst = moved[i][:, g, :].rearrange("p (f c) -> p f c", c=C)
+            src = bank[:].rearrange("p (c f) -> p f c", c=C)
+            if on_vector:
+                nc.vector.tensor_scalar(out=dst, in0=src, scalar1=cols[:, g : g + 1], scalar2=None, op0=ALU.mult)
+            else:
+                nc.scalar.activation(out=dst, in_=src, func=ACT.Copy, scale=cols[:, g : g + 1])
+
+        def quantize_moved(i):
+            codes = kept(f"moved_codes{i}", [P, BANK], U32)
+            scales = kept(f"moved_scales{i}", [P, BANK], U8)
+            quantize(codes[:], scales[:], moved[i][:].rearrange("p g w -> p (g w)"))
+            moved_q[i] = (codes, scales)
+
+        rest_banks = {}
+        rest_rows = {}
+        rest_grouped = [kept(f"rest_grouped{g}", [P, S * 4], BF16) for g in range(GROUPS)]
+        rest_codes = [kept(f"rest_codes{g}", [P, S], U32) for g in range(GROUPS)]
+        rest_scales = [kept(f"rest_scales{g}", [P, S], U8) for g in range(GROUPS)]
+
+        def decode(u):
+            g = u // 2
+            for k in range(2):
+                m0 = P * (2 * (u % 2) + k)
+                bank = next_bank()
+                for lp in range(L_PASSES):
+                    nc.tensor.matmul_mx(
+                        out=bank[:],
+                        lhsT=z_words[:, lp, 2 * m0 : 2 * (m0 + P)].bitcast(FP4X4),
+                        lhsT_scale=z_scales[:, lp, m0 : m0 + P],
+                        rhs=d_words[g][:, lp, :].bitcast(FP4X4),
+                        rhs_scale=d_scales[:, lp, BANK * g : BANK * (g + 1)],
+                        start=(lp == 0),
+                        stop=(lp == L_PASSES - 1),
+                    )
+                rest_banks[u, k] = bank
+
+        def add_template(u):
+            g = u // 2
+            for k in range(2):
+                rows = rotating("rest_rows", 2 * u + k, [P, BANK], BF16, 8)
+                nc.vector.tensor_tensor(
+                    out=rows[:].rearrange("m (u p e) -> m u p e", u=2, e=2),
+                    in0=rest_banks[u, k][:].rearrange("m (p u e) -> m u p e", u=2, e=2),
+                    in1=templ_rows[g // 2][:, g % 2, :].rearrange("m (u p e) -> m u p e", u=2, e=2),
+                    op=ALU.add,
+                )
+                rest_rows[u, k] = rows
+
+        def turn_rest(u):
+            bank = next_bank()
+            for k in range(2):
+                words = rest_rows[u, k][:].bitcast(F32)
+                for w in range(2):
+                    col = P * (2 * k + w)
+                    nc.tensor.transpose(bank[:, col : col + P], words[:, P * w : P * (w + 1)], ident[:])
+            half = rest_grouped[u // 2][:].bitcast(F32)[:, BANK * (u % 2) : BANK * (u % 2 + 1)]
+            nc.scalar.copy(
+                out=half.rearrange("p (k m w) -> p k m w", k=2, w=2),
+                in_=bank[:].rearrange("p (k w m) -> p k m w", k=2, w=2),
+            )
+
+        def quantize_rest(g):
+            quantize(rest_codes[g][:], rest_scales[g][:], rest_grouped[g][:])
+
+        def moments(i, on_vector):
+            bank = next_bank()
+            for g in range(GROUPS):
+                f = slice(P * g, P * (g + 1))
+                nc.tensor.matmul_mx(
+                    out=bank[:],
+                    lhsT=moved_q[i][0][:, f].bitcast(FP8X4),
+                    lhsT_scale=moved_q[i][1][:, f],
+                    rhs=rest_codes[g][:].bitcast(FP8X4),
+                    rhs_scale=rest_scales[g][:],
+                    start=(g == 0),
+                    stop=(g == GROUPS - 1),
+                )
+            result = rotating("result", i, [P, S], F32, 4)
+            bias = cols[:, GROUPS + i : GROUPS + i + 1]
+            if on_vector:
+                nc.vector.tensor_scalar(out=result[:], in0=bank[:], scalar1=bias, scalar2=None, op0=ALU.add)
+            else:
+                nc.scalar.activation(out=result[:], in_=bank[:], func=ACT.Identity, bias=bias)
+            nc.sync.dma_start(out=out[P * i : P * (i + 1), :], in_=result[:])
+
+        def on_scalar(n):
+            return n // C in (1, 2) and n % C in (0, 1)
+
+        turn_skin(0)
+        for n in range(3):
+            interleave(n, False)
+        quantize_skin(0)
+        interleave(3, False)
+        turn_mass_and_shift()
+        turn_skin(1)
+        quantize_bones(0)
+        quantize_skin(1)
+        spread_template(0)
+        nu = nt = nq = n3 = nqm = 0
+        nil = 4
+        for h in range(2 * TILES):
+            i, half = divmod(h, 2)
+            for g in (2 * half, 2 * half + 1):
+                blend(i, g, (h >= 18 and g == 3) or (h >= 22 and g == 1))
+            if h == 4:
+                spread_template(1)
+            if half == 0:
+                if i + 1 < TILES:
+                    while nil < 4 * ((i + 1) // 2 + 1):
+                        interleave(nil, on_scalar(nil))
+                        nil = nil + 1
+                    quantize_bones(i + 1)
+            elif i > 0:
+                quantize_moved(i - 1)
+                nqm = i
+            if nq < 4:
+                prev = nu
+                fresh = []
+                if h >= 1 and nu < UNITS and (h - 1) % 2 == 0:
+                    for n in range(2):
+                        if nu < UNITS:
+                            decode(nu)
+                            fresh.append(nu)
+                            nu = nu + 1
+                while nt < prev:
+                    turn_rest(nt)
+                    nt = nt + 1
+                for u in fresh:
+                    add_template(u)
+                while nq < 4 and nt >= 2 * nq + 2 + 1 or (nt == 8 and nq < 4 and prev == 8 and not fresh):
+                    quantize_rest(nq)
+                    nq = nq + 1
+            else:
+                for n in range(1):
+                    if n3 < nqm - 1:
+                        moments(n3, False)
+                        n3 = n3 + 1
+            if nil < 24 and nil < h + 5:
+                interleave(nil, on_scalar(nil))
+                nil = nil + 1
+        quantize_moved(TILES - 1)
+        while n3 < TILES:
+            moments(n3, n3 % 2 == 0)
+            n3 = n3 + 1

@@ -3,8 +3,8 @@ from contextlib import ExitStack
 import concourse.mybir as mybir
 from concourse.masks import make_identity
 
-V, C, J, F, L, S = 512, 4, 512, 1536, 1024, 512
-FLOPS = 2 * V * J * C * F + 2 * L * C * V * S + 2 * C * V * F * S
+VERTICES, COORDS, BONES, POSE_ROWS, MODES, SUBJECTS = 512, 4, 512, 1536, 1024, 512
+FLOPS = 2 * VERTICES * COORDS * (BONES * POSE_ROWS + MODES * SUBJECTS + POSE_ROWS * SUBJECTS)
 
 F32 = mybir.dt.float32
 BF16 = mybir.dt.bfloat16
@@ -17,14 +17,20 @@ ACT = mybir.ActivationFunctionType
 ALU = mybir.AluOpType
 
 P = 128
+PACK = 4
 BANK = 512
-N_BANKS = 8
-GROUPS = V // P
-TILES = F // P
+BANKS = 8
+GROUPS = VERTICES // P
+TILES = POSE_ROWS // P
+MODE_PASSES = MODES // (P * PACK)
+SUBJECT_TILES = SUBJECTS // P
 CHUNK = 2 * P
-CHUNKS = F // CHUNK
-L_PASSES = L // (4 * P)
-UNITS = 2 * GROUPS
+CHUNKS = POSE_ROWS // CHUNK
+PIECES = CHUNKS * COORDS
+
+PIECE_LEAD = 6
+SCALAR_CHUNKS = range(1, 4)
+VECTOR_BLEND_FROM = 9
 
 
 def tile_skinned_mass_moments_s12_kernel(
@@ -41,7 +47,7 @@ def tile_skinned_mass_moments_s12_kernel(
 
         def next_bank():
             n = len(banks_taken)
-            bank = psum.tile([P, BANK], F32, name=f"bank{n}", tag=f"bank{n % N_BANKS}")
+            bank = psum.tile([P, BANK], F32, name=f"bank{n}", tag=f"bank{n % BANKS}")
             banks_taken.append(bank)
             return bank
 
@@ -54,36 +60,37 @@ def tile_skinned_mass_moments_s12_kernel(
         def quantize(codes, scales, values):
             nc.vector.quantize_mx(out=codes.bitcast(FP8X4), scales=scales, in_=values)
 
-        z_scales = kept("z_scales", [P, L_PASSES, S], U8)
-        d_scales = kept("d_scales", [P, L_PASSES, C * V], U8)
+        z_scales = kept("z_scales", [P, MODE_PASSES, SUBJECTS], U8)
+        d_scales = kept("d_scales", [P, MODE_PASSES, COORDS * VERTICES], U8)
         nc.vector.memset(z_scales[:].bitcast(I32), 0)
         nc.vector.memset(d_scales[:].bitcast(I32), 0)
         ident = kept("ident", [P, P], F32)
         make_identity(nc, ident[:])
-        rows_f32 = kept("rows_f32", [P, P], F32)
-        nc.gpsimd.memset(rows_f32[:], 0.0)
+        vector_rows_f32 = kept("vector_rows_f32", [P, P], F32)
+        nc.gpsimd.memset(vector_rows_f32[:], 0.0)
 
-        skin_raw = [kept(f"skin_raw{h}", [P, 2, J], BF16) for h in range(2)]
-        bones_raw = [[kept(f"bones_raw{ch}_{c}", [P, 4, CHUNK], BF16) for c in range(C)] for ch in range(CHUNKS)]
-        rows_bf = kept("rows_bf", [GROUPS + TILES, P], BF16)
-        templ_cols = kept("templ_cols", [P, GROUPS, C], BF16)
-        z_words = kept("z_words", [P, L_PASSES, 2 * S], U8)
-        d_words = [kept(f"d_words{g}", [P, L_PASSES, 2 * BANK], U8) for g in range(GROUPS)]
-        bones_view = bones.rearrange("(p t) (c f) -> p t c f", t=4, c=C)
+        skin_raw = [kept(f"skin_raw{pair}", [P, 2, BONES], BF16) for pair in range(2)]
+        bones_raw = [kept(f"bones_raw{n}", [P, PACK, CHUNK], BF16) for n in range(PIECES)]
+        vector_rows = kept("vector_rows", [GROUPS + TILES, P], BF16)
+        template_cols = kept("template_cols", [P, GROUPS, COORDS], BF16)
+        z_words = kept("z_words", [P, MODE_PASSES, 2 * SUBJECTS], U8)
+        d_words = [kept(f"d_words{g}", [P, MODE_PASSES, 2 * BANK], U8) for g in range(GROUPS)]
+        bones_view = bones.rearrange("(p t) (c f) -> p t c f", t=PACK, c=COORDS)
 
-        def load_skin(h):
-            nc.sync.dma_start(
-                out=skin_raw[h][:], in_=skin[2 * P * h : 2 * P * (h + 1), :].rearrange("(g p) j -> p g j", p=P)
-            )
+        def load_skin(pair):
+            rows = skin[2 * P * pair : 2 * P * (pair + 1), :]
+            nc.sync.dma_start(out=skin_raw[pair][:], in_=rows.rearrange("(g v) j -> v g j", v=P))
 
-        def load_bones(ch):
-            for c in range(C):
-                nc.sync.dma_start(out=bones_raw[ch][c][:], in_=bones_view[:, :, c, CHUNK * ch : CHUNK * (ch + 1)])
+        def load_bones(chunk):
+            for c in range(COORDS):
+                nc.sync.dma_start(
+                    out=bones_raw[COORDS * chunk + c][:], in_=bones_view[:, :, c, CHUNK * chunk : CHUNK * (chunk + 1)]
+                )
 
-        def load_scale_rows(plane, rows):
+        def load_scale_rows(scales, rows):
             for q in range(4):
                 nc.sync.dma_start(
-                    out=plane[32 * q : 32 * q + 4].bitcast(I32),
+                    out=scales[32 * q : 32 * q + 4].bitcast(I32),
                     in_=rows.bitcast(I32)[:, 4 * q : 4 * q + 4, :].rearrange("l r n -> r l n"),
                 )
 
@@ -93,78 +100,69 @@ def tile_skinned_mass_moments_s12_kernel(
                 in_=basis_words.bitcast(I32)[:, :, 256 * g : 256 * (g + 1)].rearrange("l p n -> p l n"),
             )
 
-        def load_small():
-            nc.scalar.dma_start(out=rows_bf[0:GROUPS, :], in_=mass.rearrange("(g p) -> g p", p=P))
-            nc.scalar.dma_start(out=rows_bf[GROUPS:, :], in_=shift.rearrange("(i p) -> i p", p=P))
-            nc.scalar.dma_start(out=templ_cols[:], in_=template.rearrange("(g p c) -> p g c", p=P, c=C))
-
-        def load_codes():
-            load_scale_rows(z_scales, codes_scales)
-            nc.sync.dma_start(out=z_words[:].bitcast(I32), in_=codes_words.bitcast(I32).rearrange("l p n -> p l n"))
-            load_scale_rows(d_scales, basis_scales)
-
         load_skin(0)
-        load_small()
+        nc.scalar.dma_start(out=vector_rows[0:GROUPS, :], in_=mass.rearrange("(g v) -> g v", v=P))
+        nc.scalar.dma_start(out=vector_rows[GROUPS:, :], in_=shift.rearrange("(i f) -> i f", f=P))
+        nc.scalar.dma_start(out=template_cols[:], in_=template.rearrange("(g v c) -> v g c", v=P, c=COORDS))
         load_bones(0)
         load_skin(1)
-        load_codes()
+        load_scale_rows(z_scales, codes_scales)
+        nc.sync.dma_start(out=z_words[:].bitcast(I32), in_=codes_words.bitcast(I32).rearrange("l p n -> p l n"))
+        load_scale_rows(d_scales, basis_scales)
         load_basis(0)
         load_bones(1)
-        load_basis(1)
-        load_basis(2)
-        load_basis(3)
-        load_bones(2)
-        load_bones(3)
-        load_bones(4)
-        load_bones(5)
+        for g in range(1, GROUPS):
+            load_basis(g)
+        for chunk in range(2, CHUNKS):
+            load_bones(chunk)
 
-        skin_grouped = [kept(f"skin_grouped{h}", [P, 2 * P * 4], BF16) for h in range(2)]
-        skin_codes = [kept(f"skin_codes{h}", [P, 2 * P], U32) for h in range(2)]
-        skin_scales = [kept(f"skin_scales{h}", [P, 2 * P], U8) for h in range(2)]
+        skin_grouped = [kept(f"skin_grouped{pair}", [P, 2 * P * PACK], BF16) for pair in range(2)]
+        skin_codes = [kept(f"skin_codes{pair}", [P, 2 * P], U32) for pair in range(2)]
+        skin_scales = [kept(f"skin_scales{pair}", [P, 2 * P], U8) for pair in range(2)]
 
-        def turn_skin(h):
+        def turn_skin(pair):
             bank = next_bank()
-            words = skin_raw[h][:].bitcast(F32)
+            words = skin_raw[pair][:].bitcast(F32)
             for g in range(2):
                 for u in range(2):
                     col = P * (2 * g + u)
                     nc.tensor.transpose(bank[:, col : col + P], words[:, g, u : 2 * P : 2], ident[:])
             nc.scalar.copy(
-                out=skin_grouped[h][:].bitcast(F32).rearrange("p (g v u) -> p g v u", g=2, u=2),
+                out=skin_grouped[pair][:].bitcast(F32).rearrange("p (g v u) -> p g v u", g=2, u=2),
                 in_=bank[:].rearrange("p (g u v) -> p g v u", g=2, u=2),
             )
 
-        def quantize_skin(h):
-            quantize(skin_codes[h][:], skin_scales[h][:], skin_grouped[h][:])
+        def quantize_skin(pair):
+            quantize(skin_codes[pair][:], skin_scales[pair][:], skin_grouped[pair][:])
 
-        cols = kept("cols", [P, GROUPS + TILES], F32)
+        vector_cols = kept("vector_cols", [P, GROUPS + TILES], F32)
 
         def turn_mass_and_shift():
-            nc.scalar.copy(out=rows_f32[0 : GROUPS + TILES, :], in_=rows_bf[:])
+            nc.scalar.copy(out=vector_rows_f32[0 : GROUPS + TILES, :], in_=vector_rows[:])
             bank = next_bank()
-            nc.tensor.transpose(bank[:, 0:P], rows_f32[:], ident[:])
-            nc.scalar.copy(out=cols[:], in_=bank[:, 0 : GROUPS + TILES])
+            nc.tensor.transpose(bank[:, 0:P], vector_rows_f32[:], ident[:])
+            nc.scalar.copy(out=vector_cols[:], in_=bank[:, 0 : GROUPS + TILES])
 
-        templ_rows = [kept(f"templ_rows{h}", [P, 2, BANK], BF16) for h in range(2)]
+        template_rows = [kept(f"template_rows{pair}", [P, 2, BANK], BF16) for pair in range(2)]
 
-        def spread_template(h):
+        def spread_template(pair):
             bank = next_bank()
-            words = templ_cols[:].rearrange("p g c -> p (g c)").bitcast(F32)
+            words = template_cols[:].rearrange("v g c -> v (g c)").bitcast(F32)
             for n in range(4):
-                w = 4 * h + n
+                w = 4 * pair + n
                 nc.tensor.transpose(bank[:, P * n : P * (n + 1)], words[:, w : w + 1].to_broadcast([P, P]), ident[:])
-            nc.scalar.copy(out=templ_rows[h][:].rearrange("p g k -> p (g k)").bitcast(F32), in_=bank[:])
+            nc.scalar.copy(out=template_rows[pair][:].rearrange("m g k -> m (g k)").bitcast(F32), in_=bank[:])
 
-        grouped = {}
+        bones_grouped = {}
         bones_q = {}
 
-        def interleave(n, on_scalar):
-            ch, c = divmod(n, C)
+        def interleave(n):
+            chunk, c = divmod(n, COORDS)
             if c == 0:
-                grouped[ch] = rotating("grouped", ch, [P, 2, C, P * 4], BF16, 3)
-            dst = grouped[ch][:, :, c, :].rearrange("p i (f t) -> p i f t", t=4)
-            src = bones_raw[ch][c][:].rearrange("p t (i f) -> p i f t", i=2)
-            if on_scalar:
+                bones_grouped[chunk] = rotating("bones_grouped", chunk, [P, 2, COORDS, P * PACK], BF16, 3)
+            dst = bones_grouped[chunk][:, :, c, :].rearrange("p i (a b t) -> p i a t b", b=4, t=PACK)
+            src = bones_raw[n][:].rearrange("p t (i a b) -> p i a t b", i=2, b=4)
+            if chunk in SCALAR_CHUNKS and c % 2 == 0:
                 nc.scalar.copy(out=dst, in_=src)
             else:
                 nc.vector.tensor_copy(out=dst, in_=src)
@@ -172,15 +170,16 @@ def tile_skinned_mass_moments_s12_kernel(
         def quantize_bones(i):
             codes = rotating("bones_codes", i, [P, BANK], U32, 4)
             scales = rotating("bones_scales", i, [P, BANK], U8, 4)
-            quantize(codes[:], scales[:], grouped[i // 2][:, i % 2].rearrange("p c w -> p (c w)"))
+            quantize(codes[:], scales[:], bones_grouped[i // 2][:, i % 2].rearrange("p c w -> p (c w)"))
             bones_q[i] = (codes, scales)
 
         moved = {}
-        moved_q = {}
+        moved_codes = [kept(f"moved_codes{i}", [P, GROUPS * P], U32) for i in range(TILES)]
+        moved_scales = [kept(f"moved_scales{i}", [P, GROUPS * P], U8) for i in range(TILES)]
 
-        def blend(i, g, on_vector):
+        def blend(i, g):
             if g == 0:
-                moved[i] = rotating("moved", i, [P, GROUPS, BANK], BF16, 3)
+                moved[i] = rotating("moved", i, [P, GROUPS, BANK], BF16, 4)
             bank = next_bank()
             v = slice(P * (g % 2), P * (g % 2 + 1))
             nc.tensor.matmul_mx(
@@ -192,147 +191,151 @@ def tile_skinned_mass_moments_s12_kernel(
                 start=True,
                 stop=True,
             )
-            dst = moved[i][:, g, :].rearrange("p (f c) -> p f c", c=C)
-            src = bank[:].rearrange("p (c f) -> p f c", c=C)
-            if on_vector:
-                nc.vector.tensor_scalar(out=dst, in0=src, scalar1=cols[:, g : g + 1], scalar2=None, op0=ALU.mult)
+            dst = moved[i][:, g, :].rearrange("v (f c) -> v f c", c=COORDS)
+            src = bank[:].rearrange("v (c f) -> v f c", c=COORDS)
+            factor = vector_cols[:, g : g + 1]
+            if g == 0 and i >= VECTOR_BLEND_FROM:
+                nc.vector.tensor_scalar(out=dst, in0=src, scalar1=factor, scalar2=None, op0=ALU.mult)
             else:
-                nc.scalar.activation(out=dst, in_=src, func=ACT.Copy, scale=cols[:, g : g + 1])
+                nc.scalar.activation(out=dst, in_=src, func=ACT.Copy, scale=factor)
 
-        def quantize_moved(i):
-            codes = kept(f"moved_codes{i}", [P, BANK], U32)
-            scales = kept(f"moved_scales{i}", [P, BANK], U8)
-            quantize(codes[:], scales[:], moved[i][:].rearrange("p g w -> p (g w)"))
-            moved_q[i] = (codes, scales)
+        def quantize_moved(i, first_group, groups):
+            w = slice(P * first_group, P * (first_group + groups))
+            values = moved[i][:, first_group : first_group + groups, :].rearrange("v g w -> v (g w)")
+            quantize(moved_codes[i][:, w], moved_scales[i][:, w], values)
 
-        rest_banks = {}
         rest_rows = {}
-        rest_grouped = [kept(f"rest_grouped{g}", [P, S * 4], BF16) for g in range(GROUPS)]
-        rest_codes = [kept(f"rest_codes{g}", [P, S], U32) for g in range(GROUPS)]
-        rest_scales = [kept(f"rest_scales{g}", [P, S], U8) for g in range(GROUPS)]
+        rest_grouped = [kept(f"rest_grouped{g}", [P, SUBJECTS * PACK], BF16) for g in range(GROUPS)]
+        rest_codes = [kept(f"rest_codes{g}", [P, SUBJECTS], U32) for g in range(GROUPS)]
+        rest_scales = [kept(f"rest_scales{g}", [P, SUBJECTS], U8) for g in range(GROUPS)]
 
-        def decode(u):
-            g = u // 2
-            for k in range(2):
-                m0 = P * (2 * (u % 2) + k)
+        def decode_rest(g):
+            sums = []
+            for mt in range(SUBJECT_TILES):
                 bank = next_bank()
-                for lp in range(L_PASSES):
+                for lp in range(MODE_PASSES):
                     nc.tensor.matmul_mx(
                         out=bank[:],
-                        lhsT=z_words[:, lp, 2 * m0 : 2 * (m0 + P)].bitcast(FP4X4),
-                        lhsT_scale=z_scales[:, lp, m0 : m0 + P],
+                        lhsT=z_words[:, lp, 2 * P * mt : 2 * P * (mt + 1)].bitcast(FP4X4),
+                        lhsT_scale=z_scales[:, lp, P * mt : P * (mt + 1)],
                         rhs=d_words[g][:, lp, :].bitcast(FP4X4),
                         rhs_scale=d_scales[:, lp, BANK * g : BANK * (g + 1)],
                         start=(lp == 0),
-                        stop=(lp == L_PASSES - 1),
+                        stop=(lp == MODE_PASSES - 1),
                     )
-                rest_banks[u, k] = bank
-
-        def add_template(u):
-            g = u // 2
-            for k in range(2):
-                rows = rotating("rest_rows", 2 * u + k, [P, BANK], BF16, 8)
+                sums.append(bank)
+            for mt in range(SUBJECT_TILES):
+                rows = rotating("rest_rows", SUBJECT_TILES * g + mt, [P, BANK], BF16, 2 * SUBJECT_TILES)
                 nc.vector.tensor_tensor(
-                    out=rows[:].rearrange("m (u p e) -> m u p e", u=2, e=2),
-                    in0=rest_banks[u, k][:].rearrange("m (p u e) -> m u p e", u=2, e=2),
-                    in1=templ_rows[g // 2][:, g % 2, :].rearrange("m (u p e) -> m u p e", u=2, e=2),
+                    out=rows[:].rearrange("m (u v e) -> m u v e", u=2, e=2),
+                    in0=sums[mt][:].rearrange("m (v u e) -> m u v e", u=2, e=2),
+                    in1=template_rows[g // 2][:, g % 2, :].rearrange("m (u v e) -> m u v e", u=2, e=2),
                     op=ALU.add,
                 )
-                rest_rows[u, k] = rows
+                rest_rows[g, mt] = rows
 
-        def turn_rest(u):
-            bank = next_bank()
-            for k in range(2):
-                words = rest_rows[u, k][:].bitcast(F32)
-                for w in range(2):
-                    col = P * (2 * k + w)
-                    nc.tensor.transpose(bank[:, col : col + P], words[:, P * w : P * (w + 1)], ident[:])
-            half = rest_grouped[u // 2][:].bitcast(F32)[:, BANK * (u % 2) : BANK * (u % 2 + 1)]
-            nc.scalar.copy(
-                out=half.rearrange("p (k m w) -> p k m w", k=2, w=2),
-                in_=bank[:].rearrange("p (k w m) -> p k m w", k=2, w=2),
-            )
+        def turn_rest(g):
+            for first in range(0, SUBJECT_TILES, 2):
+                bank = next_bank()
+                for mt in range(2):
+                    words = rest_rows[g, first + mt][:].bitcast(F32)
+                    for u in range(2):
+                        col = P * (2 * mt + u)
+                        nc.tensor.transpose(bank[:, col : col + P], words[:, P * u : P * (u + 1)], ident[:])
+                dst = rest_grouped[g][:].bitcast(F32)[:, 2 * P * first : 2 * P * (first + 2)]
+                nc.scalar.copy(
+                    out=dst.rearrange("v (mt m u) -> v mt m u", mt=2, u=2),
+                    in_=bank[:].rearrange("v (mt u m) -> v mt m u", mt=2, u=2),
+                )
 
         def quantize_rest(g):
             quantize(rest_codes[g][:], rest_scales[g][:], rest_grouped[g][:])
 
-        def moments(i, on_vector):
+        def moment_pass(acc, i, g, m):
+            f = slice(P * g, P * (g + 1))
+            nc.tensor.matmul_mx(
+                out=acc,
+                lhsT=moved_codes[i][:, f].bitcast(FP8X4),
+                lhsT_scale=moved_scales[i][:, f],
+                rhs=rest_codes[g][:, m].bitcast(FP8X4),
+                rhs_scale=rest_scales[g][:, m],
+                start=(g == 0),
+                stop=(g == GROUPS - 1),
+            )
+
+        def shift_and_store(acc, result, i, m, on_vector):
+            bias = vector_cols[:, GROUPS + i : GROUPS + i + 1]
+            if on_vector:
+                nc.vector.tensor_scalar(out=result, in0=acc, scalar1=bias, scalar2=None, op0=ALU.add)
+            else:
+                nc.scalar.activation(out=result, in_=acc, func=ACT.Identity, bias=bias)
+            nc.sync.dma_start(out=out[P * i : P * (i + 1), m], in_=result)
+
+        def moments(i):
             bank = next_bank()
             for g in range(GROUPS):
-                f = slice(P * g, P * (g + 1))
-                nc.tensor.matmul_mx(
-                    out=bank[:],
-                    lhsT=moved_q[i][0][:, f].bitcast(FP8X4),
-                    lhsT_scale=moved_q[i][1][:, f],
-                    rhs=rest_codes[g][:].bitcast(FP8X4),
-                    rhs_scale=rest_scales[g][:],
-                    start=(g == 0),
-                    stop=(g == GROUPS - 1),
-                )
-            result = rotating("result", i, [P, S], F32, 4)
-            bias = cols[:, GROUPS + i : GROUPS + i + 1]
-            if on_vector:
-                nc.vector.tensor_scalar(out=result[:], in0=bank[:], scalar1=bias, scalar2=None, op0=ALU.add)
-            else:
-                nc.scalar.activation(out=result[:], in_=bank[:], func=ACT.Identity, bias=bias)
-            nc.sync.dma_start(out=out[P * i : P * (i + 1), :], in_=result[:])
+                moment_pass(bank[:], i, g, slice(0, SUBJECTS))
+            result = rotating("result", i, [P, SUBJECTS], F32, 4)
+            shift_and_store(bank[:], result[:], i, slice(0, SUBJECTS), i % 2 == 0)
 
-        def on_scalar(n):
-            return n // C in (1, 2) and n % C in (0, 1)
+        def last_moments(i):
+            width = SUBJECTS // 2
+            sides = [slice(0, width), slice(width, SUBJECTS)]
+            accs = [next_bank(), next_bank()]
+            for g in range(GROUPS):
+                for side in range(2):
+                    moment_pass(accs[side][:, 0:width], i, g, sides[side])
+            for side in range(2):
+                result = kept(f"last_result{side}", [P, width], F32)
+                shift_and_store(accs[side][:, 0:width], result[:], i, sides[side], side == 1)
 
         turn_skin(0)
-        for n in range(3):
-            interleave(n, False)
+        interleave(0)
+        interleave(1)
         quantize_skin(0)
-        interleave(3, False)
+        interleave(2)
         turn_mass_and_shift()
+        spread_template(0)
+        spread_template(1)
+        interleave(3)
         turn_skin(1)
         quantize_bones(0)
+        quantize_bones(1)
         quantize_skin(1)
-        spread_template(0)
-        nu = nt = nq = n3 = nqm = 0
-        nil = 4
-        for h in range(2 * TILES):
-            i, half = divmod(h, 2)
-            for g in (2 * half, 2 * half + 1):
-                blend(i, g, (h >= 18 and g == 3) or (h >= 22 and g == 1))
-            if h == 4:
-                spread_template(1)
-            if half == 0:
-                if i + 1 < TILES:
-                    while nil < 4 * ((i + 1) // 2 + 1):
-                        interleave(nil, on_scalar(nil))
-                        nil = nil + 1
-                    quantize_bones(i + 1)
-            elif i > 0:
-                quantize_moved(i - 1)
-                nqm = i
-            if nq < 4:
-                prev = nu
-                fresh = []
-                if h >= 1 and nu < UNITS and (h - 1) % 2 == 0:
-                    for n in range(2):
-                        if nu < UNITS:
-                            decode(nu)
-                            fresh.append(nu)
-                            nu = nu + 1
-                while nt < prev:
-                    turn_rest(nt)
-                    nt = nt + 1
-                for u in fresh:
-                    add_template(u)
-                while nq < 4 and nt >= 2 * nq + 2 + 1 or (nt == 8 and nq < 4 and prev == 8 and not fresh):
-                    quantize_rest(nq)
-                    nq = nq + 1
+
+        interleaved = COORDS
+        finished = 0
+        for i in range(TILES):
+            for tile_i in {0: (0, 1), 1: ()}.get(i, (i,)):
+                blend(tile_i, 0)
+                blend(tile_i, 1)
+            if i < GROUPS:
+                decode_rest(i)
+            if 1 <= i <= GROUPS:
+                quantize_rest(i - 1)
+            if i > GROUPS and finished < i - 2:
+                moments(finished)
+                finished = finished + 1
+            while interleaved < min(PIECES, 2 * i + PIECE_LEAD + 1):
+                interleave(interleaved)
+                interleaved = interleaved + 1
+
+            blend(i, 2)
+            blend(i, 3)
+            while interleaved < min(PIECES, 2 * i + 1 + PIECE_LEAD + 1):
+                interleave(interleaved)
+                interleaved = interleaved + 1
+            if i > 0:
+                quantize_moved(i - 1, 0, GROUPS)
+            if i + 2 < TILES:
+                quantize_bones(i + 2)
+            if i < GROUPS:
+                turn_rest(i)
             else:
-                for n in range(1):
-                    if n3 < nqm - 1:
-                        moments(n3, False)
-                        n3 = n3 + 1
-            if nil < 24 and nil < h + 5:
-                interleave(nil, on_scalar(nil))
-                nil = nil + 1
-        quantize_moved(TILES - 1)
-        while n3 < TILES:
-            moments(n3, n3 % 2 == 0)
-            n3 = n3 + 1
+                moments(finished)
+                finished = finished + 1
+
+        quantize_moved(TILES - 1, 0, 2)
+        quantize_moved(TILES - 1, 2, 2)
+        moments(TILES - 2)
+        last_moments(TILES - 1)

@@ -191,8 +191,8 @@ def tile_skinned_mass_moments_s12_kernel(
                 start=True,
                 stop=True,
             )
-            dst = moved[i][:, g, :].rearrange("v (f c) -> v f c", c=COORDS)
-            src = bank[:].rearrange("v (c f) -> v f c", c=COORDS)
+            dst = moved[i][:, g, :].rearrange("v (a b c) -> v a c b", b=2, c=COORDS)
+            src = bank[:].rearrange("v (c a b) -> v a c b", b=2, c=COORDS)
             factor = vector_cols[:, g : g + 1]
             if g == 0 and i >= VECTOR_BLEND_FROM:
                 nc.vector.tensor_scalar(out=dst, in0=src, scalar1=factor, scalar2=None, op0=ALU.mult)

@@ -52,10 +52,10 @@ def tile_skinned_mass_moments_s12_kernel(
             return bank
 
         def kept(name, shape, dtype):
-            return keep.tile(shape, dtype, name=name, tag=name, align_bytes=64)
+            return keep.tile(shape, dtype, name=name, tag=name, align_bytes=256)
 
         def rotating(tag, n, shape, dtype, bufs):
-            return work.tile(shape, dtype, name=f"{tag}{n}", tag=tag, bufs=bufs, align_bytes=64)
+            return work.tile(shape, dtype, name=f"{tag}{n}", tag=tag, bufs=bufs, align_bytes=256)
 
         def quantize(codes, scales, values):
             nc.vector.quantize_mx(out=codes.bitcast(FP8X4), scales=scales, in_=values)

from contextlib import ExitStack

import concourse.mybir as mybir
from concourse.masks import make_identity

VERTICES, COORDS, BONES, POSE_ROWS, MODES, SUBJECTS = 512, 4, 512, 1536, 1024, 512
FLOPS = 2 * VERTICES * COORDS * (BONES * POSE_ROWS + MODES * SUBJECTS + POSE_ROWS * SUBJECTS)

F32 = mybir.dt.float32
BF16 = mybir.dt.bfloat16
I32 = mybir.dt.int32
U32 = mybir.dt.uint32
U8 = mybir.dt.uint8
FP8X4 = mybir.dt.float8_e4m3fn_x4
FP4X4 = mybir.dt.float4_e2m1fn_x4
ACT = mybir.ActivationFunctionType
ALU = mybir.AluOpType

P = 128
PACK = 4
BANK = 512
BANKS = 8
GROUPS = VERTICES // P
TILES = POSE_ROWS // P
MODE_PASSES = MODES // (P * PACK)
SUBJECT_TILES = SUBJECTS // P
CHUNK = 2 * P
CHUNKS = POSE_ROWS // CHUNK
PIECES = CHUNKS * COORDS

PIECE_LEAD = 6
SCALAR_CHUNKS = range(1, 4)
VECTOR_BLEND_FROM = 9


def tile_skinned_mass_moments_s12_kernel(
    tc, skin, bones, mass, basis_words, basis_scales, codes_words, codes_scales, template, shift, out
):
    nc = tc.nc
    with ExitStack() as ctx:
        keep = ctx.enter_context(tc.tile_pool(name="keep", bufs=1))
        work = ctx.enter_context(tc.tile_pool(name="work", bufs=1))
        psum = ctx.enter_context(tc.psum_pool(name="psum", bufs=1))
        ctx.enter_context(tc.manual_schedule())

        banks_taken = []

        def next_bank():
            n = len(banks_taken)
            bank = psum.tile([P, BANK], F32, name=f"bank{n}", tag=f"bank{n % BANKS}")
            banks_taken.append(bank)
            return bank

        def kept(name, shape, dtype):
            return keep.tile(shape, dtype, name=name, tag=name, align_bytes=256)

        def rotating(tag, n, shape, dtype, bufs):
            return work.tile(shape, dtype, name=f"{tag}{n}", tag=tag, bufs=bufs, align_bytes=256)

        def quantize(codes, scales, values):
            nc.vector.quantize_mx(out=codes.bitcast(FP8X4), scales=scales, in_=values)

        z_scales = kept("z_scales", [P, MODE_PASSES, SUBJECTS], U8)
        d_scales = kept("d_scales", [P, MODE_PASSES, COORDS * VERTICES], U8)
        nc.vector.memset(z_scales[:].bitcast(I32), 0)
        nc.vector.memset(d_scales[:].bitcast(I32), 0)
        ident = kept("ident", [P, P], F32)
        make_identity(nc, ident[:])
        vector_rows_f32 = kept("vector_rows_f32", [P, P], F32)
        nc.gpsimd.memset(vector_rows_f32[:], 0.0)

        skin_raw = [kept(f"skin_raw{pair}", [P, 2, BONES], BF16) for pair in range(2)]
        bones_raw = [kept(f"bones_raw{n}", [P, PACK, CHUNK], BF16) for n in range(PIECES)]
        vector_rows = kept("vector_rows", [GROUPS + TILES, P], BF16)
        template_cols = kept("template_cols", [P, GROUPS, COORDS], BF16)
        z_words = kept("z_words", [P, MODE_PASSES, 2 * SUBJECTS], U8)
        d_words = [kept(f"d_words{g}", [P, MODE_PASSES, 2 * BANK], U8) for g in range(GROUPS)]
        bones_view = bones.rearrange("(p t) (c f) -> p t c f", t=PACK, c=COORDS)

        def load_skin(pair):
            rows = skin[2 * P * pair : 2 * P * (pair + 1), :]
            nc.sync.dma_start(out=skin_raw[pair][:], in_=rows.rearrange("(g v) j -> v g j", v=P))

        def load_bones(chunk):
            for c in range(COORDS):
                nc.sync.dma_start(
                    out=bones_raw[COORDS * chunk + c][:], in_=bones_view[:, :, c, CHUNK * chunk : CHUNK * (chunk + 1)]
                )

        def load_scale_rows(scales, rows):
            for q in range(4):
                nc.sync.dma_start(
                    out=scales[32 * q : 32 * q + 4].bitcast(I32),
                    in_=rows.bitcast(I32)[:, 4 * q : 4 * q + 4, :].rearrange("l r n -> r l n"),
                )

        def load_basis(g):
            nc.sync.dma_start(
                out=d_words[g][:].bitcast(I32),
                in_=basis_words.bitcast(I32)[:, :, 256 * g : 256 * (g + 1)].rearrange("l p n -> p l n"),
            )

        load_skin(0)
        nc.scalar.dma_start(out=vector_rows[0:GROUPS, :], in_=mass.rearrange("(g v) -> g v", v=P))
        nc.scalar.dma_start(out=vector_rows[GROUPS:, :], in_=shift.rearrange("(i f) -> i f", f=P))
        nc.scalar.dma_start(out=template_cols[:], in_=template.rearrange("(g v c) -> v g c", v=P, c=COORDS))
        load_bones(0)
        load_skin(1)
        load_scale_rows(z_scales, codes_scales)
        nc.sync.dma_start(out=z_words[:].bitcast(I32), in_=codes_words.bitcast(I32).rearrange("l p n -> p l n"))
        load_scale_rows(d_scales, basis_scales)
        load_basis(0)
        load_bones(1)
        for g in range(1, GROUPS):
            load_basis(g)
        for chunk in range(2, CHUNKS):
            load_bones(chunk)

        skin_grouped = [kept(f"skin_grouped{pair}", [P, 2 * P * PACK], BF16) for pair in range(2)]
        skin_codes = [kept(f"skin_codes{pair}", [P, 2 * P], U32) for pair in range(2)]
        skin_scales = [kept(f"skin_scales{pair}", [P, 2 * P], U8) for pair in range(2)]

        def turn_skin(pair):
            bank = next_bank()
            words = skin_raw[pair][:].bitcast(F32)
            for g in range(2):
                for u in range(2):
                    col = P * (2 * g + u)
                    nc.tensor.transpose(bank[:, col : col + P], words[:, g, u : 2 * P : 2], ident[:])
            nc.scalar.copy(
                out=skin_grouped[pair][:].bitcast(F32).rearrange("p (g v u) -> p g v u", g=2, u=2),
                in_=bank[:].rearrange("p (g u v) -> p g v u", g=2, u=2),
            )

        def quantize_skin(pair):
            quantize(skin_codes[pair][:], skin_scales[pair][:], skin_grouped[pair][:])

        vector_cols = kept("vector_cols", [P, GROUPS + TILES], F32)

        def turn_mass_and_shift():
            nc.scalar.copy(out=vector_rows_f32[0 : GROUPS + TILES, :], in_=vector_rows[:])
            bank = next_bank()
            nc.tensor.transpose(bank[:, 0:P], vector_rows_f32[:], ident[:])
            nc.scalar.copy(out=vector_cols[:], in_=bank[:, 0 : GROUPS + TILES])

        template_rows = [kept(f"template_rows{pair}", [P, 2, BANK], BF16) for pair in range(2)]

        def spread_template(pair):
            bank = next_bank()
            words = template_cols[:].rearrange("v g c -> v (g c)").bitcast(F32)
            for n in range(4):
                w = 4 * pair + n
                nc.tensor.transpose(bank[:, P * n : P * (n + 1)], words[:, w : w + 1].to_broadcast([P, P]), ident[:])
            nc.scalar.copy(out=template_rows[pair][:].rearrange("m g k -> m (g k)").bitcast(F32), in_=bank[:])

        bones_grouped = {}
        bones_q = {}

        def interleave(n):
            chunk, c = divmod(n, COORDS)
            if c == 0:
                bones_grouped[chunk] = rotating("bones_grouped", chunk, [P, 2, COORDS, P * PACK], BF16, 3)
            dst = bones_grouped[chunk][:, :, c, :].rearrange("p i (a b t) -> p i a t b", b=4, t=PACK)
            src = bones_raw[n][:].rearrange("p t (i a b) -> p i a t b", i=2, b=4)
            if chunk in SCALAR_CHUNKS and c % 2 == 0:
                nc.scalar.copy(out=dst, in_=src)
            else:
                nc.vector.tensor_copy(out=dst, in_=src)

        def quantize_bones(i):
            codes = rotating("bones_codes", i, [P, BANK], U32, 4)
            scales = rotating("bones_scales", i, [P, BANK], U8, 4)
            quantize(codes[:], scales[:], bones_grouped[i // 2][:, i % 2].rearrange("p c w -> p (c w)"))
            bones_q[i] = (codes, scales)

        moved = {}
        moved_codes = [kept(f"moved_codes{i}", [P, GROUPS * P], U32) for i in range(TILES)]
        moved_scales = [kept(f"moved_scales{i}", [P, GROUPS * P], U8) for i in range(TILES)]

        def blend(i, g):
            if g == 0:
                moved[i] = rotating("moved", i, [P, GROUPS, BANK], BF16, 4)
            bank = next_bank()
            v = slice(P * (g % 2), P * (g % 2 + 1))
            nc.tensor.matmul_mx(
                out=bank[:],
                lhsT=skin_codes[g // 2][:, v].bitcast(FP8X4),
                lhsT_scale=skin_scales[g // 2][:, v],
                rhs=bones_q[i][0][:].bitcast(FP8X4),
                rhs_scale=bones_q[i][1][:],
                start=True,
                stop=True,
            )
            dst = moved[i][:, g, :].rearrange("v (a b c) -> v a c b", b=2, c=COORDS)
            src = bank[:].rearrange("v (c a b) -> v a c b", b=2, c=COORDS)
            factor = vector_cols[:, g : g + 1]
            if g == 0 and i >= VECTOR_BLEND_FROM:
                nc.vector.tensor_scalar(out=dst, in0=src, scalar1=factor, scalar2=None, op0=ALU.mult)
            else:
                nc.scalar.activation(out=dst, in_=src, func=ACT.Copy, scale=factor)

        def quantize_moved(i, first_group, groups):
            w = slice(P * first_group, P * (first_group + groups))
            values = moved[i][:, first_group : first_group + groups, :].rearrange("v g w -> v (g w)")
            quantize(moved_codes[i][:, w], moved_scales[i][:, w], values)

        rest_rows = {}
        rest_grouped = [kept(f"rest_grouped{g}", [P, SUBJECTS * PACK], BF16) for g in range(GROUPS)]
        rest_codes = [kept(f"rest_codes{g}", [P, SUBJECTS], U32) for g in range(GROUPS)]
        rest_scales = [kept(f"rest_scales{g}", [P, SUBJECTS], U8) for g in range(GROUPS)]

        def decode_rest(g):
            sums = []
            for mt in range(SUBJECT_TILES):
                bank = next_bank()
                for lp in range(MODE_PASSES):
                    nc.tensor.matmul_mx(
                        out=bank[:],
                        lhsT=z_words[:, lp, 2 * P * mt : 2 * P * (mt + 1)].bitcast(FP4X4),
                        lhsT_scale=z_scales[:, lp, P * mt : P * (mt + 1)],
                        rhs=d_words[g][:, lp, :].bitcast(FP4X4),
                        rhs_scale=d_scales[:, lp, BANK * g : BANK * (g + 1)],
                        start=(lp == 0),
                        stop=(lp == MODE_PASSES - 1),
                    )
                sums.append(bank)
            for mt in range(SUBJECT_TILES):
                rows = rotating("rest_rows", SUBJECT_TILES * g + mt, [P, BANK], BF16, 2 * SUBJECT_TILES)
                nc.vector.tensor_tensor(
                    out=rows[:].rearrange("m (u v e) -> m u v e", u=2, e=2),
                    in0=sums[mt][:].rearrange("m (v u e) -> m u v e", u=2, e=2),
                    in1=template_rows[g // 2][:, g % 2, :].rearrange("m (u v e) -> m u v e", u=2, e=2),
                    op=ALU.add,
                )
                rest_rows[g, mt] = rows

        def turn_rest(g):
            for first in range(0, SUBJECT_TILES, 2):
                bank = next_bank()
                for mt in range(2):
                    words = rest_rows[g, first + mt][:].bitcast(F32)
                    for u in range(2):
                        col = P * (2 * mt + u)
                        nc.tensor.transpose(bank[:, col : col + P], words[:, P * u : P * (u + 1)], ident[:])
                dst = rest_grouped[g][:].bitcast(F32)[:, 2 * P * first : 2 * P * (first + 2)]
                nc.scalar.copy(
                    out=dst.rearrange("v (mt m u) -> v mt m u", mt=2, u=2),
                    in_=bank[:].rearrange("v (mt u m) -> v mt m u", mt=2, u=2),
                )

        def quantize_rest(g):
            quantize(rest_codes[g][:], rest_scales[g][:], rest_grouped[g][:])

        def moment_pass(acc, i, g, m):
            f = slice(P * g, P * (g + 1))
            nc.tensor.matmul_mx(
                out=acc,
                lhsT=moved_codes[i][:, f].bitcast(FP8X4),
                lhsT_scale=moved_scales[i][:, f],
                rhs=rest_codes[g][:, m].bitcast(FP8X4),
                rhs_scale=rest_scales[g][:, m],
                start=(g == 0),
                stop=(g == GROUPS - 1),
            )

        def shift_and_store(acc, result, i, m, on_vector):
            bias = vector_cols[:, GROUPS + i : GROUPS + i + 1]
            if on_vector:
                nc.vector.tensor_scalar(out=result, in0=acc, scalar1=bias, scalar2=None, op0=ALU.add)
            else:
                nc.scalar.activation(out=result, in_=acc, func=ACT.Identity, bias=bias)
            nc.sync.dma_start(out=out[P * i : P * (i + 1), m], in_=result)

        def moments(i):
            bank = next_bank()
            for g in range(GROUPS):
                moment_pass(bank[:], i, g, slice(0, SUBJECTS))
            result = rotating("result", i, [P, SUBJECTS], F32, 4)
            shift_and_store(bank[:], result[:], i, slice(0, SUBJECTS), i % 2 == 0)

        def last_moments(i):
            width = SUBJECTS // 2
            sides = [slice(0, width), slice(width, SUBJECTS)]
            accs = [next_bank(), next_bank()]
            for g in range(GROUPS):
                for side in range(2):
                    moment_pass(accs[side][:, 0:width], i, g, sides[side])
            for side in range(2):
                result = kept(f"last_result{side}", [P, width], F32)
                shift_and_store(accs[side][:, 0:width], result[:], i, sides[side], side == 1)

        turn_skin(0)
        interleave(0)
        interleave(1)
        quantize_skin(0)
        interleave(2)
        turn_mass_and_shift()
        spread_template(0)
        spread_template(1)
        interleave(3)
        turn_skin(1)
        quantize_bones(0)
        quantize_bones(1)
        quantize_skin(1)

        interleaved = COORDS
        finished = 0
        for i in range(TILES):
            for tile_i in {0: (0, 1), 1: ()}.get(i, (i,)):
                blend(tile_i, 0)
                blend(tile_i, 1)
            if i < GROUPS:
                decode_rest(i)
            if 1 <= i <= GROUPS:
                quantize_rest(i - 1)
            if i > GROUPS and finished < i - 2:
                moments(finished)
                finished = finished + 1
            while interleaved < min(PIECES, 2 * i + PIECE_LEAD + 1):
                interleave(interleaved)
                interleaved = interleaved + 1

            blend(i, 2)
            blend(i, 3)
            while interleaved < min(PIECES, 2 * i + 1 + PIECE_LEAD + 1):
                interleave(interleaved)
                interleaved = interleaved + 1
            if i > 0:
                quantize_moved(i - 1, 0, GROUPS)
            if i + 2 < TILES:
                quantize_bones(i + 2)
            if i < GROUPS:
                turn_rest(i)
            else:
                moments(finished)
                finished = finished + 1

        quantize_moved(TILES - 1, 0, 2)
        quantize_moved(TILES - 1, 2, 2)
        moments(TILES - 2)
        last_moments(TILES - 1)
